import numpy as np, ml_dtypes
CORES = [40,41,42,43,44,45,46,47]
N = 8
import mx_ref
BF = ml_dtypes.bfloat16
def tile(rs):
    return np.stack(rs, axis=2).reshape(128, -1).astype(BF)
def pick(q, e):
    c = np.concatenate([q[0].reshape(128, -1, 4), np.zeros((128, 1, 4), np.uint8)], axis=1); s = np.concatenate([q[1], np.ones((16, 1), np.uint8)], axis=1)
    return (np.ascontiguousarray(c[:, e].reshape(128, -1)), np.ascontiguousarray(s[:, e]))
def join(*qs):
    return (np.concatenate([q[0] for q in qs], axis=1), np.concatenate([q[1] for q in qs], axis=1))
def put(q, e, v):
    c, s = q[0].reshape(128, -1, 4).copy(), q[1].copy(); c[:, e] = v[0].reshape(128, -1, 4); s[:, e] = v[1]
    return (c.reshape(128, -1), s)
def pk(c, s):
    return (np.ascontiguousarray(c), mx_ref.live(s))
def emit(q):
    return q[0], q[1]
def packed(v, rng):
    q = [mx_ref.quantize(np.ascontiguousarray(v[r])) for r in range(N)]
    return np.stack([a for a, b in q]), np.stack([mx_ref.plane(b, rng) for a, b in q])
def values_of_codes():
    e, c = np.zeros((128, 128, 4), np.float32), np.zeros((128, 2, 4), np.uint8)
    e[np.arange(128), np.arange(128), 0] = 1
    c[:127, :, 0] = np.arange(256).reshape(2, 128).T[:127]
    return mx_ref.matmul(mx_ref.quantize(e.reshape(128, 512).astype(BF)), (c.reshape(128, 8), np.full((16, 2), 127, np.uint8))).T.reshape(-1).astype(np.float64)
CODE_VALUE, SCALE_VALUE = values_of_codes(), 2.0 ** (np.arange(256) - 127.0)
def decode(q):
    return (CODE_VALUE[q[0]].reshape(16, 8, -1, 4) * SCALE_VALUE[q[1]][:, None, :, None] + 0.0).reshape(128, -1).astype(np.float32)
def f(rng, *shape):
    return mx_ref.flush((rng.standard_normal(shape, dtype=np.float32) * np.exp2(rng.integers(-2, 3, shape[:-1] + (1,)))).astype(BF))
def wide(rng, *shape, cols=0):
    v = rng.standard_normal(shape, dtype=np.float32) * np.exp2(rng.integers(-12, 13, shape)).astype(np.float32)
    if cols: v *= np.repeat(np.exp2(rng.integers(-cols, cols + 1, shape[:-2] + (1, shape[-1] // 4))) * (rng.random(shape[:-2] + (1, shape[-1] // 4)) > 0.0625), 4, axis=-1).astype(np.float32)
    return mx_ref.flush(v.astype(BF))
C, H = 256, 128
MASK = [1, 2, 4]
def numbers_of(rng):
    return {"x": np.array(f(rng, N, 128, 4 * C)), "u": np.array(f(rng, N, 128, 512)), "v": np.array(f(rng, N, 128, 512))}
def weights(rng, w):
    c, s = packed(np.ascontiguousarray(w).reshape(N, 128, 2048), rng)
    return {"wc": c, "ws": s}
def layers(rng, still=[], pairs=False):
    w = np.array(f(rng, N, 128, 2048)).reshape(N, 8, 16, 4, 8, 16, 4)
    for i in still:
        w[:, :, i] = 0
        w[:, :, :, :, :, i] = 0
    if pairs:
        w[:, :, :, :, :, 8:] = 0
        for g in range(8):
            w[:, g, 8, 0, g, 8, 0] = -28.0
            for b in range(4): w[:, g, 10, b, g, 9, 0] = -2.0 ** (b - 5)
    return weights(rng, w)
def setup_inputs(rng):
    return {**numbers_of(rng), **layers(rng)}
def setup_inputs_ties(rng):
    d = numbers_of(rng)
    o = rng.permutation(N)
    k = rng.integers(0, 4, (N, 8, C))
    k[o[1]] += 1
    k[o[2], rng.permutation(8)[:4]] = 1
    for g in range(8): k[o[3], g] = 1 + (rng.permutation(C) < H + g % 3 - 1)
    x = d["x"].reshape(N, 8, 16, C, 4)
    x[:, :, 0] = 0
    x[:, :, 0, :, 0] = k.astype(np.float32).astype(BF)
    a = np.exp2(rng.integers(-3, 4, (N, 8, C)).astype(np.float32))
    x[:, :, 8:] = 0
    x[:, :, 8, :, 0] = (-1.125 * a).astype(BF)
    x[:, :, 10, :, 0] = (-0.0703125 * a).astype(BF)
    u = d["u"].reshape(N, 128, 128, 4)
    u[:, :, ::16] = 0
    for r in range(N):
        for h in range(0, 128, 16): u[r, h, h, 0] = 0.0 if r == o[0] else -1.0 if r == o[1] else 1.0
    return {"x": x.reshape(N, 128, 4 * C), "u": u.reshape(N, 128, 512), "v": d["v"], **layers(rng, [0], True)}
def setup_inputs_near(rng):
    d = numbers_of(rng)
    x = d["x"].astype(np.float32).reshape(N, 8, 16, C, 4)
    x[:, :, 0] = 0
    x[:, :, 8:] = 0
    u = d["u"].reshape(N, 128, 128, 4)
    u[:, :, ::16] = 0
    o = rng.permutation(N) % 4
    for r in range(N):
        c = rng.choice([-1.0, 1.0], (8, 1))
        s = rng.integers(0, 16, (8, C))
        digits = ((s[:, :, None] >> np.arange(4)) & 1) * np.exp2(np.arange(4) - 23.0)
        if o[r] < 2:
            x[r, :, 0, :, 0] = c
            x[r, :, 8] = digits
            x[r, :, 11, :, 0] = 2.0 ** -10
        elif o[r] == 2: x[r, :, 8] = digits * rng.choice([-1.0, 1.0], (8, C, 1))
        else:
            x[r, :, 8, :, 0] = np.where(s < 8, 1.25, 0.0) * 2.0 ** -30 * c
            x[r, :, 9, :, 0] = np.where(s < 8, 0.0, 1.125) * 2.0 ** -30 * c
            for g in rng.permutation(8)[:4]:
                e = rng.choice([-1.0, 1.0], C) * 2.0 ** -30
                x[r, g, 8, :, 0] = 1.25 * e
                x[r, g, 9, :, 0] = -1.125 * e
        at = [0, C - 1, int(rng.integers(C)), int(rng.integers(C))]
        for g, j in zip(rng.permutation(8)[:4], at): x[r, g, 0, j, 0] = 2.0 ** 29 * rng.choice([-1.0, 1.0])
        k = 1.0 if o[r] == 0 else 2.0 ** -30
        for h in range(0, 128, 16):
            u[r, h, h, 0] = k if o[r] < 2 else 1.0
            if o[r] < 2: u[r, h + 11, h, 0] = k
            if o[r] < 3: u[r, h + 8, h] = k
            else:
                u[r, h + 8, h, 0] = k
                u[r, h + 9, h, 0] = 1.125 * k
    return {"x": x.reshape(N, 128, 4 * C).astype(BF), "u": u.reshape(N, 128, 512), "v": d["v"], **layers(rng, [0, 8, 9, 10, 11, 12, 13, 14, 15])}
def setup_inputs_odd(rng):
    d = numbers_of(rng)
    o = rng.permutation(N)
    x = (1.0 + (2 * rng.integers(0, 64, (N, 16, 8, C, 4)) + 1) * 2.0 ** -7) * np.exp2(-rng.integers(0, 7, (N, 16, 8, C, 4)).astype(np.float64)) * rng.choice([-1.0, 1.0], (N, 16, 8, C, 4))
    s = rng.choice([-1.0, 1.0], (N, 8, 2, C))
    late = np.arange(C) >= H
    e = np.arange(C)[None, :] - np.where(np.arange(8)[:, None] < rng.integers(1, 8), 1, 0)
    s[o[0], :, 0] = np.where(late, 1.0, -1.0)
    s[o[1], :, 0] = np.where((e >= 0) & (e < H), 1.0, -1.0)
    s[o[2], :, 0] = np.where(late[None, :] == (rng.permutation(8)[:, None] < 4), 1.0, -1.0)
    x[:, :, 0, :, 0] = 1.96875 * 2.0 ** 8 * s.reshape(N, 16, C)
    u = d["u"].reshape(N, 16, 8, 128, 4)
    u[:, :, 0, ::16] = 0
    for r in o[:3]:
        u[r, :, :, ::16] = 0
        for g in range(8): u[r, 2 * g, 0, 16 * g, 0] = 1.0
    for i, g in enumerate(rng.permutation(8)[:4]):
        x[o[3], 2 * g, 1, :, 0] = (8 + rng.integers(0, 2, C)) * 2.0 ** (i - 8)
        u[o[3], :, :, 16 * g] = 0
        u[o[3], 2 * g, 1, 16 * g, 0] = 1.0
    return {"x": x.astype(np.float32).reshape(N, 128, 4 * C).astype(BF), "u": u.reshape(N, 128, 512), "v": d["v"], **layers(rng, [0, 8])}
def setup_inputs_ends(rng):
    d = numbers_of(rng)
    x = np.zeros((N, 8, 16, C, 4))
    u = d["u"].astype(np.float32).reshape(N, 128, 128, 4)
    v = d["v"].astype(np.float32)
    w = np.zeros((N, 128, 4, 128, 4), np.float32)
    o = rng.permutation(N) % 4
    i = np.arange(128)
    for r in range(N):
        h = rng.permutation(8)
        c = np.where(h < 2, 0.0, h % 2 * 2.0 - 1.0)[None, :, None]
        low = -(0.9 + 0.1 * rng.random((8, 16, C, 4))) * 2.0 ** 30
        if o[r] == 0: x[r] = low
        if o[r] == 1: x[r] = np.where((rng.random(C) < 0.5)[:, None], (1.0 + 0.4 * rng.random((8, 16, C, 4))) * 2.0 ** 27, low)
        if o[r] == 2: x[r] = -(1.0 + 0.125 * rng.integers(0, 8, (8, 16, C, 4))) * 2.0 ** -30
        if o[r] == 3: x[r] = d["x"][r].astype(np.float32).reshape(8, 16, C, 4)[:, :, :1]
        if o[r] < 2:
            u[r, :, ::16] = c * (0.9 + 0.1 * rng.random((128, 8, 4))) * 2.0 ** 30
            v[r] = rng.choice([-1.0, 1.0], (128, 512)) * (0.9 + 0.1 * rng.random((128, 512))) * 2.0 ** 30
        if o[r] == 2:
            u[r, :, ::16] = c * (1.0 + 0.125 * rng.integers(0, 8, (128, 8, 4))) * 2.0 ** -30
            v[r] = rng.choice([-1.0, 1.0], (128, 512)) * (1.0 + 0.125 * rng.integers(0, 8, (128, 512))) * 2.0 ** -30
        if o[r] == 3: u[r, :, ::16] *= np.abs(c).astype(np.float32)
        k = np.array([4.0, 8.0, 16.0])[rng.permutation(8) % 3]
        for b in range(4): w[r, i, b, i, b] = k[i // 16]
    return {"x": x.astype(np.float32).reshape(N, 128, 4 * C).astype(BF), "u": u.reshape(N, 128, 512).astype(BF), "v": v.astype(BF), **weights(rng, w.astype(BF))}
def setup_inputs_spread(rng):
    d = setup_inputs(rng)
    d["x"] = wide(rng, N, 128, 4 * C, cols=6)
    return d
def check_inputs(d):
    b = []
    for k in ("x", "u", "v"):
        a = np.abs(d[k].astype(np.float32))
        if not (np.isfinite(a).all() and ((a == 0) | (a >= 2.0 ** -30) & (a <= 2.0 ** 30)).all()): b.append("a value of " + k)
    none, least, most = [emit(mx_ref.quantize(np.full((128, 16), k, np.float32).astype(BF)))[1][0, 0] for k in (0.0, 2.0 ** -8, 2.0 ** 8)]
    for r in range(N):
        if ((d["wc"][r] == 0x7F) | (d["wc"][r] == 0xFF)).any(): b.append("wc: a code that is no number")
        s = mx_ref.live(d["ws"][r])
        if ((s != none) & ((s < least) | (s > most))).any(): b.append("ws: a scale out of range")
    return b
def parts(t):
    return np.ascontiguousarray(t.reshape(8, 16, -1, 4).transpose(2, 0, 1, 3)).reshape(-1, 16, 4)
def laid(p):
    return np.ascontiguousarray(p.reshape(-1, 8, 16, 4).transpose(1, 2, 0, 3)).reshape(128, -1)
def layer(w, q):
    return mx_ref.quantize(tile([np.maximum(mx_ref.matmul(pick(w, np.arange(128 * b, 128 * b + 128)), q), np.float32(0.0)) * np.float32(0.03125) for b in range(4)]))
def reference(x, u, v, wc, ws):
    qu = [mx_ref.quantize(u[r]) for r in range(N)]
    lay = [pk(wc[r], ws[r]) for r in range(N)]
    now = [x[r] for r in range(N)]
    for m in MASK:
        t, high, low, own, out = [], [], [], [], []
        for r in range(N):
            q = mx_ref.quantize(now[r])
            s = mx_ref.matmul(qu[r], q)[::16] + np.float32(0.0)
            flag = np.zeros((8, C), bool)
            np.put_along_axis(flag, np.argsort(-s, axis=1, kind="stable")[:, :H], True, axis=1)
            high.append(np.flatnonzero(flag.T))
            low.append(np.flatnonzero(~flag.T))
            t.append(decode(q))
            p = parts(t[r].astype(BF))
            own.append(mx_ref.quantize(laid(p[high[r]])))
            out.append(mx_ref.quantize(laid(p[low[r]])))
        home = [layer(lay[r], own[r]) for r in range(N)]
        guest = [layer(lay[r], out[r ^ m]) for r in range(N)]
        for r in range(N):
            a = np.zeros((8 * C, 16, 4), np.float32)
            a[high[r]] = parts(decode(home[r]))
            a[low[r]] = parts(decode(guest[r ^ m]))
            now[r] = (t[r] + laid(a)).astype(BF)
    y, op = np.zeros((N, 128, C), np.float32), np.zeros((N, 8, C), np.float32)
    oc, osc = np.zeros((N, 128, 4 * C), np.uint8), np.zeros((N, 16, C), np.uint8)
    for r in range(N):
        q = mx_ref.quantize(now[r])
        y[r] = mx_ref.matmul(mx_ref.quantize(v[r]), q)
        n = np.zeros(8 * C, np.int64)
        n[high[r]] = np.arange(4 * C)
        n[low[r]] = 4 * C + np.arange(4 * C)
        op[r] = n.reshape(C, 8).T
        oc[r], osc[r] = emit(q)
    return {"y": y, "op": op, "oc": oc, "osc": osc}

from concourse.mybir import dt, AluOpType, ActivationFunctionType

OP = AluOpType
ACT = ActivationFunctionType
R = 3
F8, U8, BF, F32, I32, U16 = "float8_e4m3fn_x4", "uint8", "bfloat16", "float32", "int32", "uint16"

SCRATCH = {"ps": ("psum", [128, 4096], F32)}


def _buf(name, n, dtype):
    SCRATCH[name] = ("sbuf", [128, n], dtype)


for _n, _w, _d in [
    ("xs", 1024, BF), ("us", 512, BF), ("vs", 512, BF), ("xt", 1024, BF),
    ("ones", 1024, BF), ("eb", 1040, BF), ("kt", 512, BF), ("k0", 512, BF), ("kp", 512, BF), ("pri", 512, F32), ("prs", 512, F32),
    ("kmp", 272, I32), ("kma", 272, I32), ("mk", 272, F32), ("nm", 272, F32), ("sm", 272, F32), ("hb", 280, F32),
    ("thr", 256, F32), ("rs", 256, BF), ("idv", 256, I32),
    ("pi", 2, I32), ("pg", 2, I32), ("pj", 2, I32), ("gf", 2, F32), ("i8", 2, F32), ("pval", 2, F32), ("nph", 2, F32),
    ("pph", 2, F32), ("hcol", 2, F32), ("gcol", 2, F32), ("m64", 16, F32), ("ph", 16, F32), ("neg", 16, F32),
    ("uli", 8, I32), ("ulu", 8, U16),
    ("fl0", 1024, BF), ("fl1", 1024, BF), ("fl2", 1024, BF), ("fl3", 1024, BF), ("fl4", 1024, BF),
    ("exm", 256, BF), ("exs", 512, BF), ("cum", 32, F32), ("sg", 16, F32), ("st", 16, I32), ("t2", 16, F32), ("v1", 16, F32),
    ("v2", 16, I32), ("pos0", 16, I32), ("pos1", 16, I32), ("posu", 16, U16),
    ("so0", 16, I32), ("so1", 16, I32), ("so2", 16, I32), ("so3", 16, I32), ("so4", 16, I32), ("so5", 16, I32), ("so6", 16, I32), ("so7", 16, I32), ("sou", 16, U16),
    ("l2", 128, I32), ("la0", 32, I32), ("lb0", 16, I32), ("lc0", 8, I32), ("ld0", 8, I32), ("le0", 8, I32), ("lu0", 8, U16),
    ("la1", 32, I32), ("lb1", 16, I32), ("lc1", 8, I32), ("ld1", 8, I32), ("le1", 8, I32), ("lu1", 8, U16),
    ("win0", 2048, I32), ("win1", 2048, I32), ("win2", 2048, I32),
    ("tab1", 8192, BF), ("tab2", 8192, BF), ("ft", 512, BF), ("gt", 512, BF), ("at", 512, BF), ("bt", 512, BF),
    ("opi", 32, F32), ("opt", 32, F32), ("opn", 16, I32), ("yo", 256, F32),
]:
    _buf(_n, _w, _d)
PAIR = {}
for _n, _w, _k in [("u", 128, 1), ("ut", 128, 1), ("v", 128, 1), ("w", 512, 1), ("ex", 128, 1), ("fs", 128, 1), ("as", 128, 1),
                   ("e", 256, 4), ("f", 256, 5), ("k", 128, 3), ("x", 256, R + 1),
                   ("go", 128, R), ("gi", 128, R), ("bo", 128, R), ("bi", 128, R)]:
    _buf("q" + _n, _w * _k, F8)
    _buf("s" + _n, _w * _k, U8)
    for _j in range(_k):
        PAIR[_n + (str(_j) if _k > 1 else "")] = (_n, _w * _j)

SEMAPHORES = ["eV", "eA", "eP", "eG", "dx", "du", "dw", "dv", "dop", "dout", "rsent"] + ["%s%d" % (n, r) for n in ("lg", "lf", "ga", "ba") for r in range(R)]


def track(g, T):
    queue = {"V": g.vector, "A": g.scalar, "P": g.tensor, "G": g, "S": g.sync}
    total, known = {}, {k: {} for k in queue}
    writer, readers, order = {}, {}, [0]

    def wait(q, toks):
        for _, sem, val, snap in sorted(toks, key=lambda t: -t[0]):
            if val is None:
                val = total[sem]
            if known[q].get(sem, 0) >= val:
                continue
            queue[q].wait_ge(T.sem[sem], val)
            for k, v in snap.items():
                known[q][k] = max(known[q].get(k, 0), v)
            known[q][sem] = val

    def needs(q, reads, writes):
        toks = []
        for k in reads:
            if k in writer:
                toks.append(writer[k])
        for k in writes:
            if k in writer and not (q == "P" and writer[k][1] == "eP"):
                toks.append(writer[k])
            toks += readers.get(k, [])
        wait(q, toks)

    def note(reads, writes, tok):
        for k in reads:
            readers.setdefault(k, []).append(tok)
        for k in writes:
            writer[k] = tok
            readers[k] = []

    def op(q, name, args, reads, writes, **kw):
        needs(q, reads, writes)
        sem = "e" + q
        if q == "V":
            call = {"copy": g.vector.tensor_copy, "tt": g.vector.tensor_tensor, "ts": g.vector.tensor_scalar, "scan": g.vector.tensor_tensor_scan,
                    "quant": g.vector.quantize_mx, "fill": g.vector.memset, "turn": g.vector.transpose}[name]
        elif q == "G":
            call = {"iota": g.iota, "select": g.affine_select}[name]
        else:
            call = g.scalar.activation if q == "A" else g.tensor.matmul_mx
        call(*args, **kw).then_inc(T.sem[sem], 1)
        total[sem] = total.get(sem, 0) + 1
        order[0] += 1
        note(reads, writes, (order[0], sem, total[sem], dict(known[q])))

    def dma(q, sem, out, in_, reads, writes):
        needs(q, reads, writes)
        queue[q].dma_start(out, in_).then_inc(T.sem[sem], 16)
        total[sem] = total.get(sem, 0) + 16
        order[0] += 1
        note(reads, writes, (order[0], sem, None, dict(known[q])))

    def landing(sem, n, writes):
        total[sem] = n
        order[0] += 1
        note([], writes, (order[0], sem, n, {}))

    def finish():
        for sem, n in total.items():
            if known["G"].get(sem, 0) < n:
                g.wait_ge(T.sem[sem], n)
    return op, dma, landing, needs, finish, total


def rank_program(g, core, T, topo):
    rank = T.rank_of(core)
    if rank is None:
        return
    op, dma, landing, needs, finish, total = track(g, T)
    ps = T.ps

    def view(name, a, b):
        buf, o = PAIR[name]
        return T["q" + buf][:, o + a:o + b], T["s" + buf][:, o + a:o + b]

    def quant(name, a, b, tile_view, reads):
        op("V", "quant", view(name, a, b) + (tile_view,), reads, ["q" + name])

    def mm(bank, n, left, right, reads, start=True, stop=True):
        op("P", "mm", (ps[:, 512 * bank:512 * bank + n], left[0], left[1], right[0], right[1], start, stop), reads, ["bank%d" % bank])

    dma("S", "dx", T.xs[:], T.x[:], [], ["xs"])
    dma("A", "du", T.us[:], T.u[:], [], ["us"])
    dma("S", "dw", T.qw[:].bitcast(dt.uint8), T.wc[:], [], ["qw"])
    dma("S", "dw", T.sw[:], T.ws[:], [], ["sw"])
    dma("A", "dv", T.vs[:], T.v[:], [], ["vs"])

    op("G", "iota", (T.pi[:], [[0, 2]], 0, 1), [], ["pi"])
    op("G", "iota", (T.kmp[:], [[1, 272]], 128, -1), [], ["kmp"])
    op("G", "iota", (T.m64[:], [[64, 16]], 0, 0), [], ["m64"], allow_small_or_imprecise_dtypes=True)
    op("G", "iota", (T.uli[:], [[16, 8]], 0, 0), [], ["uli"])
    op("V", "fill", (T.ones[:], 1.0), [], ["ones"])
    op("G", "select", (T.eb[:, 4:1028], T.ones[:], [[0, 2], [-1, 128], [1000, 4]], OP.is_equal, 0.0, 0, 1), ["ones"], ["eb"])
    op("V", "ts", (T.pg[:], T.pi[:], 4, None, OP.arith_shift_right), ["pi"], ["pg"])
    op("V", "ts", (T.pj[:], T.pi[:], 15, None, OP.bitwise_and), ["pi"], ["pj"])
    op("V", "ts", (T.gf[:], T.pg[:], 1.0, None, OP.mult), ["pg"], ["gf"])
    op("V", "ts", (T.i8[:], T.pj[:], 8.0, None, OP.mult), ["pj"], ["i8"])
    op("V", "tt", (T.pval[:], T.i8[:], T.gf[:], OP.add), ["i8", "gf"], ["pval"])
    op("V", "ts", (T.kma[:], T.kmp[:], 15, None, OP.bitwise_and), ["kmp"], ["kma"])
    op("V", "ts", (T.mk[:], T.kma[:], 0.0, None, OP.is_equal), ["kma"], ["mk"])
    op("V", "ts", (T.nm[:], T.kma[:], 0.0, None, OP.not_equal), ["kma"], ["nm"])
    op("V", "copy", (T.ulu[:], T.uli[:]), ["uli"], ["ulu"])
    op("V", "fill", (T.hb[:, 0:1], -5e29), [], ["hb0"])
    op("V", "fill", (T.neg[:], -64.0), [], ["neg"])
    op("V", "fill", (T.fl4[:], 0.0), [], ["fl4"])
    op("V", "fill", (T.eb[:, 0:4], 0.0), [], ["ebl"])
    op("V", "fill", (T.eb[:, 1028:1040], 0.0), [], ["ebr"])
    op("V", "fill", (T.exs[:, 256:512], 0.0), [], ["exz"])
    quant("u", 0, 128, T.us[:], ["us"])
    op("V", "copy", (T.qut[:].bitcast(dt.uint32), T.qu[:].bitcast(dt.uint32).indirect(T.ulu[:])), ["qu", "ulu"], ["qut"])
    op("V", "copy", (T.sut[:], T.su[:].indirect(T.ulu[:])), ["qu", "ulu"], ["sut"])
    quant("x0", 0, 256, T.xs[:], ["xs"])
    for out, in_, scale, bias, key, need in [
            (T.sm[:, 256:272], T.mk[:, 256:272], -5e29, 0.0, "smx", ["mk"]), (T.thr[:], T.mk[:, 0:256], 128.5, -1.0, "thr", ["mk"]),
            (T.hcol[:], T.gf[:], -256.0, 2048.0, "hcol", ["gf"]), (T.gcol[:], T.gf[:], -1024.0, 8192.0, "gcol", ["gf"]),
            (T.nph[:], T.pval[:], -0.5, 0.0, "nph", ["pval"]), (T.pph[:], T.pval[:], 512.5, 0.0, "pph", ["pval"]), (T.cum[:, 0:1], T.pval[:, 0:1], -0.5, 0.0, "cum0", ["pval"]),
            (T.ph[:], T.m64[:], 1025.0, T.pph[:, 0:1], "ph", ["m64", "pph"])]:
        op("A", "act", (out, in_, ACT.Identity), need, [key], scale=scale, bias=bias)
    op("G", "iota", (T.pri[:], [[1, 8], [8, 16], [1000, 4]], -3000, 0), [], ["pri"], allow_small_or_imprecise_dtypes=True)
    op("A", "act", (T.prs[:], T.pri[:], ACT.Sign), ["pri", "nph"], ["prs"], scale=0.5, bias=T.nph[:, 0:1])
    op("A", "act", (T.kp[:], T.prs[:], ACT.Relu), ["prs"], ["kp"])
    op("G", "select", (T.k0[:], T.ones[:, 0:512], [[-16, 8], [0, 16], [0, 4]], OP.is_ge, 0.0, 0, 1), ["ones"], ["k0"])
    op("G", "select", (T.k0[:], T.k0[:], [[16, 8], [0, 16], [0, 4]], OP.is_ge, 0.0, 15, -1), ["k0"], ["k0"])
    op("G", "select", (T.rs[:], T.ones[:, 0:256], [[0, 16], [1, 16]], OP.not_equal, 0.0, 0, 0), ["ones"], ["rs"])
    op("G", "iota", (T.idv[:], [[1, 256]], 0, 16), [], ["idv"])
    op("G", "select", (T.kt[:], T.ones[:, 0:512], [[0, 128], [1, 4]], OP.is_equal, 0.0, -3, 0), ["ones"], ["kt"])
    op("G", "iota", (T.win0[:], [[0, 2048]], 0, 0), [], ["win0"])

    def late(k):
        if k in (1, 2):
            for b in ((0, 1), (2, 3))[k - 1]:
                quant("e%d" % b, 0, 256, T.eb[:, 4 - b:1028 - b], ["eb", "ebl", "ebr"])
        if k == 3:
            quant("k1", 0, 128, T.k0[:], ["k0"])
            quant("k2", 0, 128, T.kp[:], ["kp"])
            quant("k0", 0, 128, T.kt[:], ["kt"])

    turn = [0]

    def bank():
        turn[0] += 1
        return 2 + turn[0] % 6

    def out_of_psum(q, out, k, n, writes, relu=False):
        src = ps[:, 512 * k:512 * k + n]
        if q == "V":
            if relu:
                op("V", "ts", (out, src, 0.0, 0.03125, OP.max, OP.mult), ["bank%d" % k], writes)
            else:
                op("V", "copy", (out, src), ["bank%d" % k], writes)
        elif relu:
            op("A", "act", (out, src, ACT.Relu), ["bank%d" % k], writes, scale=0.03125)
        else:
            op("A", "act", (out, src, ACT.Copy), ["bank%d" % k], writes)

    def table1(r, i):
        b, d = divmod(i, 8)
        k = bank()
        mm(k, 256, view("e%d" % b, 16 * d, 16 * d + 128), view("x%d" % r, 0, 256), ["qe%d" % b, "qx%d" % r])
        out_of_psum("A", T.tab1[:, 2048 * b + 256 * d:2048 * b + 256 * d + 256], k, 256, ["t1_%d_%d" % (b, d)])

    def table2(src, half, i, q):
        b, d = divmod(i, 8)
        k = bank()
        a = 2048 * b + 256 * d + 128 * half
        mm(k, 128, view("e%d" % b, 16 * d, 16 * d + 128), view(src, 0, 128), ["qe%d" % b, "q" + src])
        out_of_psum(q, T.tab2[:, a:a + 128], k, 128, ["t2_%d_%d_%d" % (b, d, half)])

    def layer(src, tile_name, dst):
        ks = []
        for b in range(4):
            k = bank()
            mm(k, 128, view("w", 128 * b, 128 * b + 128), view(src, 0, 128), ["qw", "sw", "q" + src])
            ks.append(k)
        for b in (0, 2, 1, 3):
            out_of_psum("V" if b < 2 else "A", T[tile_name][:, b:512:4], ks[b], 128, [tile_name + str(b)], relu=True)
        quant(dst, 0, 128, T[tile_name][:], [tile_name + str(b) for b in range(4)])

    def send(src, dst, sem, to):
        rid, pid, _ = topo.addr(to)
        needs("G", ["q" + src], [])
        m = topo.mask(core, to)
        n = len(topo.engines(core, to))
        there, here = view(dst, 0, 128), view(src, 0, 128)
        g.remote_dma(there[0].bitcast(dt.uint8), here[0].bitcast(dt.uint8), T.sem[sem], T.sem.rsent, pid, rid, m)
        g.remote_dma(there[1], here[1], T.sem[sem], T.sem.rsent, pid, rid, m)
        total["rsent"] = total.get("rsent", 0) + 2 * n
        return 2 * n

    def slots(t):
        f = T["fl%d" % t]
        for s in ([16] if t == 4 else range(4 * t, 4 * t + 4)):
            b = s % 4
            if s == 16:
                op("V", "tt", (f[:, b:1024:4], ps[:, 0:256], T.hb[:, 17:273], OP.is_lt), ["bank0", "hb"], ["fl%d_%d" % (t, s)])
                continue
            op("V", "tt", (f[:, 64 * s + b:1024:4], ps[:, 16 * s:256], T.hb[:, 0:256 - 16 * s], OP.is_le), ["bank0", "hb", "hb0"], ["fl%d_%d" % (t, s)])
            if s:
                op("V", "tt", (f[:, b:64 * s:4], ps[:, 0:16 * s], T.hb[:, 273 - 16 * s:273], OP.is_lt), ["bank0", "hb"], ["fl%d_%dl" % (t, s)])

    def count(t):
        keys = ["fl4", "fl4_16"] if t == 4 else [x for s in range(4 * t, 4 * t + 4) for x in ("fl%d_%d" % (t, s), "fl%d_%dl" % (t, s))]
        quant("f%d" % t, 0, 256, T["fl%d" % t][:], keys)

    def count_mm(t, start, stop):
        mm(1, 256, view("k1", 0, 128), view("f%d" % t, 0, 256), ["qk1", "qf%d" % t], start, stop)

    def gather(st, tile_name):
        lu = "lu%d" % st
        for b in (0, 2, 1, 3):
            win = T.tab1[:, 2048 * b:2048 * b + 2048].indirect(T[lu][:, 0:8])
            reads = [lu] + ["t1_%d_%d" % (b, d) for d in range(8)]
            if b < 2:
                op("V", "copy", (T[tile_name][:, b:512:4], win), reads, [tile_name + str(b)])
            else:
                op("A", "act", (T[tile_name][:, b:512:4], win, ACT.Copy), reads, [tile_name + str(b)])

    def make_list(st):
        o, s = 64 * st, str(st)
        src = ["l2_%d_%d" % (st, k) for k in range(8)]
        op("V", "tt", (T["la" + s][:], T.l2[:, o:o + 32], T.l2[:, o + 32:o + 64], OP.add), src, ["la" + s])
        op("V", "tt", (T["lb" + s][:], T["la" + s][:, 0:16], T["la" + s][:, 16:32], OP.add), ["la" + s], ["lb" + s])
        op("V", "tt", (T["lc" + s][:], T["lb" + s][:, 0:8], T["lb" + s][:, 8:16], OP.add), ["lb" + s], ["lc" + s])
        op("V", "ts", (T["ld" + s][:], T["lc" + s][:], T.hcol[:, 0:1], None, OP.add), ["lc" + s, "hcol"], ["ld" + s])
        op("V", "ts", (T["le" + s][:], T["ld" + s][:], 2047, None, OP.bitwise_and), ["ld" + s], ["le" + s])
        op("V", "copy", (T["lu" + s][:], T["le" + s][:]), ["le" + s], ["lu" + s])

    for r in range(R):
        partner = T.cores[rank ^ (1 << r)]
        win = "win%d" % r
        qx = "qx%d" % r
        mm(0, 256, view("ut", 0, 128), view("x%d" % r, 0, 256), ["qut", "sut", qx])
        op("V", "tt", (T.sm[:, 0:256], ps[:, 0:256], T.mk[:, 0:256], OP.mult), ["bank0", "mk"], ["sm"])
        op("V", "scan", (T.hb[:, 1:273], T.nm[:], T.sm[:], -5e29, OP.mult, OP.add), ["nm", "sm", "smx"], ["hb"])
        for k, (t, done) in enumerate(((4, None), (0, 4), (1, 0), (2, 1), (3, 2))):
            if r == 0:
                late(k)
            slots(t)
            if done is not None:
                count(done)
        count(3)
        i = 0
        for upto, t in ((10, 4), (14, 0), (18, 1), (22, 2), (26, 3)):
            while i < upto:
                table1(r, i)
                i += 1
            count_mm(t, t == 4, t == 3)
        op("V", "tt", (T.exm[:], ps[:, 512:768], T.thr[:], OP.is_lt), ["bank1", "thr"], ["exm"])
        op("V", "scan", (T.exs[:, 0:256], T.rs[:], T.exm[:], 0.0, OP.mult, OP.add), ["rs", "exm"], ["exs"])
        quant("ex", 0, 128, T.exs[:], ["exs", "exz"])
        mm(0, 128, view("k0", 0, 128), view("ex", 0, 128), ["qk0", "qex"])
        mm(1, 128, view("k2", 0, 128), view("ex", 0, 128), ["qk2", "qex"])
        while i < 32:
            table1(r, i)
            i += 1
        op("V", "ts", (T.sg[:], T.exs[:, 15:256:16], 2050.0, -1025.0, OP.mult, OP.add), ["exs"], ["sg"])
        op("V", "ts", (T.st[:], T.exs[:, 15:256:16], -1024.0, 1024.0, OP.mult, OP.add), ["exs"], ["st"])
        op("V", "scan", (T.cum[:, 1:17], T.neg[:], ps[:, 3:64:4], T.nph[:, 0:1], OP.add, OP.add), ["neg", "bank0", "nph"], ["cum"])
        op("V", "tt", (T.t2[:], ps[:, 515:576:4], T.cum[:, 0:16], OP.add), ["bank1", "cum", "cum0"], ["t2"])
        op("V", "tt", (T.v1[:], T.t2[:], T.sg[:], OP.mult), ["t2", "sg"], ["v1"])
        op("V", "tt", (T.v2[:], T.v1[:], T.ph[:], OP.add), ["v1", "ph"], ["v2"])
        op("V", "ts", (T.pos0[:], T.v2[:], 3, 1023, OP.arith_shift_right, OP.bitwise_and), ["v2"], ["pos0"])
        op("V", "tt", (T.pos1[:], T.pos0[:], T.st[:], OP.add), ["pos0", "st"], ["pos1"])
        op("V", "copy", (T.posu[:], T.pos1[:]), ["pos1"], ["posu"])
        op("V", "copy", (T[win][:, 0:2048].indirect(T.posu[:]), T.idv[:]), ["posu", "idv"], [win])
        for st in (1, 0):
            for k in range(8):
                dma("S", ("lf%d", "lg%d")[st] % r, T.l2[:, 64 * st + 8 * k:64 * st + 8 * k + 8],
                    T[win][16 * k:16 * k + 1, 1024 * st:1024 * st + 1024], [win], ["l2_%d_%d" % (st, k)])
        op("V", "ts", (T.so0[:], T.v2[:], 9, 112, OP.arith_shift_right, OP.bitwise_and), ["v2"], ["so0"])
        op("V", "ts", (T.so1[:], T.v2[:], 6, 15, OP.arith_shift_right, OP.bitwise_and), ["v2"], ["so1"])
        op("V", "ts", (T.so2[:], T.v2[:], T.gcol[:, 0:1], None, OP.add), ["v2", "gcol"], ["so2"])
        op("V", "ts", (T.so3[:], T.st[:], 3, None, OP.arith_shift_right), ["st"], ["so3"])
        op("V", "ts", (T.so4[:], T.so2[:], 2, 1792, OP.arith_shift_right, OP.bitwise_and), ["so2"], ["so4"])
        op("V", "tt", (T.so5[:], T.so0[:], T.so1[:], OP.add), ["so0", "so1"], ["so5"])
        op("V", "tt", (T.so6[:], T.so3[:], T.so4[:], OP.add), ["so3", "so4"], ["so6"])
        op("V", "tt", (T.so7[:], T.so5[:], T.so6[:], OP.add), ["so5", "so6"], ["so7"])
        op("V", "copy", (T.sou[:], T.so7[:]), ["so7"], ["sou"])
        if r == R - 1:
            op("V", "fill", (T.opi[:, 16:32], 0.0), [], ["opz"])
            op("V", "ts", (T.opn[:], T.v2[:], 1023, None, OP.bitwise_and), ["v2"], ["opn"])
            op("V", "tt", (T.opi[:, 0:16], T.opn[:], T.st[:], OP.add), ["opn", "st"], ["opi"])
            op("V", "turn", (T.opt[:], T.opi[:]), ["opi", "opz"], ["opt"])
            for k in range(8):
                a, e = divmod(k, 2)
                dma("S", "dop", T.op[k:k + 1, :], T.opt[32 * a:32 * a + 16, 16 * e:16 * e + 16], ["opt"], [])
        make_list(1)
        gather(1, "gt")
        quant("go%d" % r, 0, 128, T.gt[:], ["gt%d" % b for b in range(4)])
        n = send("go%d" % r, "gi%d" % r, "ga%d" % r, partner)
        landing("ga%d" % r, n, ["qgi%d" % r])
        if r + 1 < R:
            op("G", "iota", (T["win%d" % (r + 1)][:], [[0, 2048]], 0, 0), [], ["win%d" % (r + 1)])
        make_list(0)
        gather(0, "ft")
        quant("fs", 0, 128, T.ft[:], ["ft%d" % b for b in range(4)])
        layer("fs", "at", "as")
        if r == 0:
            quant("v", 0, 128, T.vs[:], ["vs"])
        for i in range(8):
            table2("as", 0, i, "VA"[i % 2])
        layer("gi%d" % r, "bt", "bo%d" % r)
        n = send("bo%d" % r, "bi%d" % r, "ba%d" % r, partner)
        for i in range(8, 32):
            table2("as", 0, i, "VA"[i % 2])
        landing("ba%d" % r, n, ["qbi%d" % r])
        for i in range(32):
            table2("bi%d" % r, 1, i, "A" if i >= 26 else "VA"[i % 2])
        for b in range(4):
            op("V", "tt", (T.xt[:, b:1024:4], T.tab2[:, 2048 * b:2048 * b + 2048].indirect(T.sou[:]), T.tab1[:, 2048 * b:2048 * b + 256], OP.add),
               ["sou", "t1_%d_0" % b] + ["t2_%d_%d_%d" % (b, d, h) for d in range(8) for h in (0, 1)], ["xt%d" % b])
        quant("x%d" % (r + 1), 0, 256, T.xt[:], ["xt%d" % b for b in range(4)])

    dma("S", "dout", T.oc[:], view("x3", 0, 256)[0].bitcast(dt.uint8), ["qx3"], [])
    mm(0, 256, view("v", 0, 128), view("x3", 0, 256), ["qv", "qx3"])
    op("V", "copy", (T.yo[:], ps[:, 0:256]), ["bank0"], ["yo"])
    for k in range(4):
        dma("A", "dout", T.osc[4 * k:4 * k + 4, :], T.sx[32 * k:32 * k + 4, 256 * R:256 * R + 256], ["qx3"], [])
    dma("S", "dout", T.y[:], T.yo[:], ["yo"], [])
    finish()
